import numpy as np
import ml_dtypes


def mxq(x, axis, fmt="e4m3"):
    dtype, down = {"e4m3": (ml_dtypes.float8_e4m3fn, 7), "e5m2": (ml_dtypes.float8_e5m2, 14)}[fmt]
    v = np.moveaxis(np.asarray(x, np.float32).astype(ml_dtypes.bfloat16).astype(np.float64), axis, -1)
    blocks = v.reshape(v.shape[:-1] + (-1, 32))
    amax = np.abs(blocks).max(-1, keepdims=True)
    byte = np.maximum(np.where(amax > 0, np.frexp(amax)[1] - 1 + 127, 0) - down, 1)
    scale = np.exp2(byte - 127.0)
    codes = (blocks / scale).astype(np.float32).astype(dtype).astype(np.float64)
    return np.moveaxis((codes * scale).reshape(v.shape), -1, axis)


WIDE = False


def mx_kscale(k):
    if not WIDE:
        return np.ones(k)
    levels = np.array([10, -10, 5, -5, 0])
    if k % 512:
        return np.exp2(np.random.permutation(np.resize(levels, k // 32))).repeat(32)
    a = np.empty((k // 512, 16))
    for p in range(k // 512):
        a[p, :8] = np.random.permutation(np.resize(levels, 8))
        for g in range(8):
            far = levels[np.abs(levels - a[p, g]) >= 10]
            a[p, g + 8] = far[np.random.randint(len(far))]
    return np.exp2(a.ravel()).repeat(32)


def f64(x):
    return np.asarray(x).astype(np.float64)


def striped(idx):
    return np.tile(idx.reshape(-1, 16).T, (8, 1)).astype(np.uint16)


def unstriped(offs):
    return offs[:16].T.reshape(-1).astype(np.int64)


def gelu(v):
    return 0.5 * v * (1.0 + np.tanh(np.sqrt(2.0 / np.pi) * (v + 0.044715 * v**3)))


K, T, S, N, U = 1024, 1024, 512, 128, 1024
P = 2 ** 7


def setup_inputs():
    n = np.random.standard_normal
    s = mx_kscale(K)[:, None]
    return {
        "xT": (n((K, T)) * s).astype(np.float32),
        "gate": np.tile(np.random.uniform(0.5, 1.5, S), (P, 1)).astype(np.float32),
        "w1": (n((K, N)) / np.sqrt(K) / s).astype(np.float32),
        "offs": striped(np.random.permutation(T)[:S]),
        "dst": striped(np.random.permutation(U)[:S]),
    }


def reference(xT, gate, w1, offs, dst):
    xq = mxq(f64(xT)[:, unstriped(offs)], 0, "e4m3")
    y = gelu(mxq(f64(w1), 0, "e4m3").T @ xq)
    out = np.zeros((N, U))
    out[:, unstriped(dst)] = y * f64(gate)[:1]
    return out

@@ -1,0 +1,145 @@
+from contextlib import ExitStack
+
+import concourse.mybir as mybir
+
+K, T, S, N, U = 1024, 1024, 512, 128, 1024
+FLOPS = 2 * K * S * N
+
+F32 = mybir.dt.float32
+BF16 = mybir.dt.bfloat16
+I32 = mybir.dt.int32
+U32 = mybir.dt.uint32
+U16 = mybir.dt.uint16
+U8 = mybir.dt.uint8
+FP8X4 = mybir.dt.float8_e4m3fn_x4
+COPY = mybir.ActivationFunctionType.Copy
+GELU = mybir.ActivationFunctionType.Gelu_apprx_tanh
+MULT = mybir.AluOpType.mult
+
+P = 128
+PACK = 4
+K_PASS = P * PACK
+PASSES = K // K_PASS
+GROUP = 16
+CHUNKS = (((512, 256), (256, 128), (256, 128)), ((256, 256), (256, 128), (256, 128), (128, 64), (128, 64)))
+PIECES = (256, 256)
+PLANE_ROW = (4, 0)
+
+
+def interleave(nc, engine, dst, src):
+    d = dst.rearrange("p (c i) t -> p c t i", i=4)
+    s = src.rearrange("p t (c i) -> p c t i", i=4)
+    if engine == "scalar":
+        nc.scalar.activation(d, s, COPY)
+    else:
+        nc.vector.tensor_copy(d, s)
+
+
+def tile_picked_route2_lingelu_e_kernel(tc, xT, gate, w1, offs, dst, out):
+    nc = tc.nc
+    with ExitStack() as ctx:
+        keep = ctx.enter_context(tc.tile_pool(name="keep", bufs=1))
+        psum = ctx.enter_context(tc.psum_pool(name="psum", bufs=1))
+
+        offs_t = keep.tile([P, S // GROUP], U16, name="offs_t")
+        dst_t = keep.tile([P, S // GROUP], U16, name="dst_t")
+        window = keep.tile([P, U], F32, name="window", align_bytes=64)
+        all_scales = keep.tile([P, T], U8, name="all_scales", align_bytes=64)
+        all_words = [keep.tile([P, T], U32, name=f"all_words{g}", align_bytes=64) for g in range(PASSES)]
+
+        warm = keep.tile([P, 8], F32, name="warm")
+        warm_out = keep.tile([P, 8], F32, name="warm_out")
+        nc.vector.memset(warm[:], 0.0)
+        nc.scalar.activation(warm_out[:], warm[:], GELU)
+        nc.vector.memset(all_scales[:].bitcast(I32), 0)
+        nc.vector.memset(window[:], 0.0)
+
+        raw = {}
+        for g in range(PASSES):
+            rows = xT[g * K_PASS : (g + 1) * K_PASS, :].rearrange("(p j) t -> p j t", j=PACK)
+            t0 = 0
+            for c, (n, ns) in enumerate(CHUNKS[g]):
+                raw[g, c] = keep.tile([P, PACK, n], F32, name=f"raw{g}_{c}", align_bytes=64)
+                nc.sync.dma_start(raw[g, c][:], rows[:, :, t0 : t0 + n])
+                if g == 0 and c == 0:
+                    nc.sync.dma_start(offs_t[:], offs)
+                t0 = t0 + n
+        w_raw = []
+        for g in range(PASSES):
+            w_raw.append(keep.tile([P, PACK, N], F32, name=f"w_raw{g}", align_bytes=64))
+            nc.sync.dma_start(w_raw[g][:], w1[g * K_PASS : (g + 1) * K_PASS, :].rearrange("(p j) m -> p j m", j=PACK))
+        gate_t = keep.tile([P, S], F32, name="gate_t", align_bytes=64)
+        nc.sync.dma_start(gate_t[:], gate)
+        nc.sync.dma_start(dst_t[:], dst)
+
+        starts = [sum(PIECES[:h]) for h in range(len(PIECES))]
+        words = {}
+        scales = {}
+
+        def lists(tile, h):
+            return tile[:, starts[h] // GROUP : (starts[h] + PIECES[h]) // GROUP]
+
+        for g in range(PASSES):
+            t0 = 0
+            for c, (n, ns) in enumerate(CHUNKS[g]):
+                grouped = keep.tile([P, n, PACK], BF16, name=f"grouped{g}_{c}", align_bytes=64)
+                if ns > 0:
+                    interleave(nc, "scalar", grouped[:, n - ns : n, :], raw[g, c][:, :, n - ns : n])
+                if ns < n:
+                    interleave(nc, "vector", grouped[:, 0 : n - ns, :], raw[g, c][:, :, 0 : n - ns])
+                nc.vector.quantize_mx(
+                    out=all_words[g][:, t0 : t0 + n].bitcast(FP8X4),
+                    scales=all_scales[PLANE_ROW[g] : P, t0 : t0 + n],
+                    in_=grouped[:].rearrange("p c t -> p (c t)"),
+                )
+                t0 = t0 + n
+            if g == 0:
+                words0 = keep.tile([P, S], U32, name="words0", align_bytes=64)
+                nc.vector.tensor_copy(words0[:], all_words[0][:].indirect(offs_t[:]))
+
+        w_words = []
+        w_scales = []
+
+        def weights(g):
+            w_grouped = keep.tile([P, N, PACK], BF16, name=f"w_grouped{g}", align_bytes=64)
+            interleave(nc, "scalar", w_grouped[:], w_raw[g][:])
+            w_words.append(keep.tile([P, N], U32, name=f"w_words{g}", align_bytes=64))
+            w_scales.append(keep.tile([P, N], U8, name=f"w_scales{g}", align_bytes=64))
+            nc.vector.quantize_mx(
+                out=w_words[g][:].bitcast(FP8X4),
+                scales=w_scales[g][:],
+                in_=w_grouped[:].rearrange("p m t -> p (m t)"),
+            )
+
+        for h, n in enumerate(PIECES):
+            scales[h] = keep.tile([P, n], U8, name=f"scales{h}", align_bytes=64)
+            words[h] = keep.tile([P, n], U32, name=f"words1_{h}", align_bytes=64)
+            nc.vector.tensor_copy(words[h][:], all_words[1][:].indirect(lists(offs_t, h)))
+            if h == 0:
+                weights(0)
+            nc.vector.tensor_copy(scales[h][:], all_scales[:].indirect(lists(offs_t, h)))
+            if h == 0:
+                weights(1)
+
+        ys = []
+        for h, n in enumerate(PIECES):
+            acc = psum.tile([P, n], F32, name=f"acc{h}")
+            for g in range(PASSES):
+                moving = words0[:, starts[h] : starts[h] + n] if g == 0 else words[h][:]
+                nc.tensor.matmul_mx(
+                    out=acc[:],
+                    lhsT=w_words[g][:].bitcast(FP8X4),
+                    lhsT_scale=w_scales[g][:],
+                    rhs=moving.bitcast(FP8X4),
+                    rhs_scale=scales[h][PLANE_ROW[g] : P, :],
+                    start=(g == 0),
+                    stop=(g == PASSES - 1),
+                )
+            y = keep.tile([P, n], F32, name=f"y{h}", align_bytes=64)
+            nc.scalar.activation(y[:], acc[:], GELU)
+            ys.append(y)
+        for h, n in enumerate(PIECES):
+            nc.vector.tensor_tensor(
+                window[:].indirect(lists(dst_t, h)), ys[h][:], gate_t[:, starts[h] : starts[h] + n], MULT
+            )
+        nc.sync.dma_start(out, window[:])

@@ -20,126 +20,136 @@ P = 128
 PACK = 4
 K_PASS = P * PACK
 PASSES = K // K_PASS
-GROUP = 16
-CHUNKS = (((512, 256), (256, 128), (256, 128)), ((256, 256), (256, 128), (256, 128), (128, 64), (128, 64)))
-PIECES = (256, 256)
-PLANE_ROW = (4, 0)
+LIST_ROWS = 16
+SCALE_ROW = (4, 0)
+HALF = S // 2
+QUANT = 256
+RUN = 4
+W_RAW_BYTES = PACK * N * 4
+
+CHUNKS = (((512, 256), (512, 192)), ((512, 320), (256, 128), (256, 128)))
 
 
-def interleave(nc, engine, dst, src):
-    d = dst.rearrange("p (c i) t -> p c t i", i=4)
-    s = src.rearrange("p t (c i) -> p c t i", i=4)
-    if engine == "scalar":
-        nc.scalar.activation(d, s, COPY)
+def round_and_interleave(nc, on_scalar, grouped, rows):
+    target = grouped.rearrange("p (c i) t -> p c t i", i=RUN)
+    source = rows.rearrange("p t (c i) -> p c t i", i=RUN)
+    if on_scalar:
+        nc.scalar.activation(target, source, COPY)
     else:
-        nc.vector.tensor_copy(d, s)
+        nc.vector.tensor_copy(target, source)
+
+
+def quantise(nc, words, scales, grouped):
+    nc.vector.quantize_mx(out=words.bitcast(FP8X4), scales=scales, in_=grouped.rearrange("p c t -> p (c t)"))
+
+
+def list_half(list_tile, h):
+    return list_tile[:, h * HALF // LIST_ROWS : (h + 1) * HALF // LIST_ROWS]
 
 
 def tile_picked_route2_lingelu_e_kernel(tc, xT, gate, w1, offs, dst, out):
     nc = tc.nc
     with ExitStack() as ctx:
         keep = ctx.enter_context(tc.tile_pool(name="keep", bufs=1))
+        reused = ctx.enter_context(tc.tile_pool(name="reused", bufs=1))
         psum = ctx.enter_context(tc.psum_pool(name="psum", bufs=1))
 
-        offs_t = keep.tile([P, S // GROUP], U16, name="offs_t")
-        dst_t = keep.tile([P, S // GROUP], U16, name="dst_t")
-        window = keep.tile([P, U], F32, name="window", align_bytes=64)
+        offs_t = keep.tile([P, S // LIST_ROWS], U16, name="offs_t")
+        dst_t = keep.tile([P, S // LIST_ROWS], U16, name="dst_t")
+        placed = keep.tile([P, U], F32, name="placed", align_bytes=64)
         all_scales = keep.tile([P, T], U8, name="all_scales", align_bytes=64)
         all_words = [keep.tile([P, T], U32, name=f"all_words{g}", align_bytes=64) for g in range(PASSES)]
 
-        warm = keep.tile([P, 8], F32, name="warm")
-        warm_out = keep.tile([P, 8], F32, name="warm_out")
-        nc.vector.memset(warm[:], 0.0)
-        nc.scalar.activation(warm_out[:], warm[:], GELU)
         nc.vector.memset(all_scales[:].bitcast(I32), 0)
-        nc.vector.memset(window[:], 0.0)
+        nc.vector.memset(placed[:], 0.0)
 
-        raw = {}
+        x_raw = {}
         for g in range(PASSES):
             rows = xT[g * K_PASS : (g + 1) * K_PASS, :].rearrange("(p j) t -> p j t", j=PACK)
-            t0 = 0
-            for c, (n, ns) in enumerate(CHUNKS[g]):
-                raw[g, c] = keep.tile([P, PACK, n], F32, name=f"raw{g}_{c}", align_bytes=64)
-                nc.sync.dma_start(raw[g, c][:], rows[:, :, t0 : t0 + n])
-                if g == 0 and c == 0:
+            first = 0
+            for tokens, scalar_share in CHUNKS[g]:
+                x_raw[g, first] = keep.tile([P, PACK, tokens], F32, name=f"x_raw{g}_{first}", align_bytes=64)
+                nc.sync.dma_start(x_raw[g, first][:], rows[:, :, first : first + tokens])
+                if (g, first) == (0, 0):
                     nc.sync.dma_start(offs_t[:], offs)
-                t0 = t0 + n
+                first = first + tokens
         w_raw = []
         for g in range(PASSES):
-            w_raw.append(keep.tile([P, PACK, N], F32, name=f"w_raw{g}", align_bytes=64))
+            w_raw.append(reused.tile([P, PACK, N], F32, name=f"w_raw{g}", align_bytes=64, offset=g * W_RAW_BYTES))
             nc.sync.dma_start(w_raw[g][:], w1[g * K_PASS : (g + 1) * K_PASS, :].rearrange("(p j) m -> p j m", j=PACK))
         gate_t = keep.tile([P, S], F32, name="gate_t", align_bytes=64)
         nc.sync.dma_start(gate_t[:], gate)
         nc.sync.dma_start(dst_t[:], dst)
 
-        starts = [sum(PIECES[:h]) for h in range(len(PIECES))]
-        words = {}
-        scales = {}
-
-        def lists(tile, h):
-            return tile[:, starts[h] // GROUP : (starts[h] + PIECES[h]) // GROUP]
-
+        x_grouped = [keep.tile([P, T, PACK], BF16, name=f"x_grouped{g}", align_bytes=64) for g in range(PASSES)]
+        picked_words0 = keep.tile([P, S], U32, name="picked_words0", align_bytes=64)
         for g in range(PASSES):
-            t0 = 0
-            for c, (n, ns) in enumerate(CHUNKS[g]):
-                grouped = keep.tile([P, n, PACK], BF16, name=f"grouped{g}_{c}", align_bytes=64)
-                if ns > 0:
-                    interleave(nc, "scalar", grouped[:, n - ns : n, :], raw[g, c][:, :, n - ns : n])
-                if ns < n:
-                    interleave(nc, "vector", grouped[:, 0 : n - ns, :], raw[g, c][:, :, 0 : n - ns])
-                nc.vector.quantize_mx(
-                    out=all_words[g][:, t0 : t0 + n].bitcast(FP8X4),
-                    scales=all_scales[PLANE_ROW[g] : P, t0 : t0 + n],
-                    in_=grouped[:].rearrange("p c t -> p (c t)"),
-                )
-                t0 = t0 + n
+            first = 0
+            for tokens, scalar_share in CHUNKS[g]:
+                grouped = x_grouped[g][:, first : first + tokens, :]
+                split = tokens - scalar_share
+                round_and_interleave(nc, True, grouped[:, split:tokens, :], x_raw[g, first][:, :, split:tokens])
+                for a in range(0, split, QUANT):
+                    b = min(a + QUANT, split)
+                    round_and_interleave(nc, False, grouped[:, a:b, :], x_raw[g, first][:, :, a:b])
+                for a in range(first, first + tokens, QUANT):
+                    cols = slice(a, a + QUANT)
+                    quantise(nc, all_words[g][:, cols], all_scales[SCALE_ROW[g] : P, cols], x_grouped[g][:, cols, :])
+                first = first + tokens
             if g == 0:
-                words0 = keep.tile([P, S], U32, name="words0", align_bytes=64)
-                nc.vector.tensor_copy(words0[:], all_words[0][:].indirect(offs_t[:]))
+                nc.vector.tensor_copy(picked_words0[:], all_words[0][:].indirect(offs_t[:]))
 
         w_words = []
         w_scales = []
 
-        def weights(g):
+        def quantise_weights(g):
             w_grouped = keep.tile([P, N, PACK], BF16, name=f"w_grouped{g}", align_bytes=64)
-            interleave(nc, "scalar", w_grouped[:], w_raw[g][:])
+            round_and_interleave(nc, True, w_grouped[:], w_raw[g][:])
             w_words.append(keep.tile([P, N], U32, name=f"w_words{g}", align_bytes=64))
             w_scales.append(keep.tile([P, N], U8, name=f"w_scales{g}", align_bytes=64))
-            nc.vector.quantize_mx(
-                out=w_words[g][:].bitcast(FP8X4),
-                scales=w_scales[g][:],
-                in_=w_grouped[:].rearrange("p m t -> p (m t)"),
-            )
+            quantise(nc, w_words[g][:], w_scales[g][:], w_grouped[:])
 
-        for h, n in enumerate(PIECES):
-            scales[h] = keep.tile([P, n], U8, name=f"scales{h}", align_bytes=64)
-            words[h] = keep.tile([P, n], U32, name=f"words1_{h}", align_bytes=64)
-            nc.vector.tensor_copy(words[h][:], all_words[1][:].indirect(lists(offs_t, h)))
-            if h == 0:
-                weights(0)
-            nc.vector.tensor_copy(scales[h][:], all_scales[:].indirect(lists(offs_t, h)))
-            if h == 0:
-                weights(1)
+        def gather_scales(h, tile):
+            nc.vector.tensor_copy(tile[:], all_scales[:].indirect(list_half(offs_t, h)))
 
-        ys = []
-        for h, n in enumerate(PIECES):
-            acc = psum.tile([P, n], F32, name=f"acc{h}")
+        def gather_words1(h, tile):
+            nc.vector.tensor_copy(tile[:], all_words[1][:].indirect(list_half(offs_t, h)))
+
+        words_bytes = HALF * 4
+        picked_scales = [
+            keep.tile([P, HALF], U8, name="picked_scales0", align_bytes=64),
+            reused.tile([P, HALF], U8, name="picked_scales1", align_bytes=64, offset=W_RAW_BYTES + words_bytes),
+        ]
+        picked_words1 = [
+            reused.tile([P, HALF], U32, name=f"picked_words1_{h}", align_bytes=64, offset=h * W_RAW_BYTES)
+            for h in range(2)
+        ]
+        gather_scales(0, picked_scales[0])
+        quantise_weights(0)
+        gather_words1(0, picked_words1[0])
+        quantise_weights(1)
+        gather_scales(1, picked_scales[1])
+        gather_words1(1, picked_words1[1])
+
+        activated = []
+        for h in range(2):
+            acc = psum.tile([P, HALF], F32, name=f"acc{h}")
+            moving = (picked_words0[:, h * HALF : (h + 1) * HALF], picked_words1[h][:])
             for g in range(PASSES):
-                moving = words0[:, starts[h] : starts[h] + n] if g == 0 else words[h][:]
                 nc.tensor.matmul_mx(
                     out=acc[:],
                     lhsT=w_words[g][:].bitcast(FP8X4),
                     lhsT_scale=w_scales[g][:],
-                    rhs=moving.bitcast(FP8X4),
-                    rhs_scale=scales[h][PLANE_ROW[g] : P, :],
+                    rhs=moving[g].bitcast(FP8X4),
+                    rhs_scale=picked_scales[h][SCALE_ROW[g] : P, :],
                     start=(g == 0),
                     stop=(g == PASSES - 1),
                 )
-            y = keep.tile([P, n], F32, name=f"y{h}", align_bytes=64)
-            nc.scalar.activation(y[:], acc[:], GELU)
-            ys.append(y)
-        for h, n in enumerate(PIECES):
+            activated.append(keep.tile([P, HALF], F32, name=f"activated{h}", align_bytes=64))
+            nc.scalar.activation(activated[h][:], acc[:], GELU)
+
+        for h in range(2):
             nc.vector.tensor_tensor(
-                window[:].indirect(lists(dst_t, h)), ys[h][:], gate_t[:, starts[h] : starts[h] + n], MULT
+                placed[:].indirect(list_half(dst_t, h)), activated[h][:], gate_t[:, h * HALF : (h + 1) * HALF], MULT
             )
-        nc.sync.dma_start(out, window[:])
+        nc.sync.dma_start(out, placed[:])

@@ -7,7 +7,6 @@ FLOPS = 2 * K * S * N
 
 F32 = mybir.dt.float32
 BF16 = mybir.dt.bfloat16
-I32 = mybir.dt.int32
 U32 = mybir.dt.uint32
 U16 = mybir.dt.uint16
 U8 = mybir.dt.uint8
@@ -20,14 +19,18 @@ P = 128
 PACK = 4
 K_PASS = P * PACK
 PASSES = K // K_PASS
+PAIRS = 2 * PASSES
 LIST_ROWS = 16
-SCALE_ROW = (4, 0)
 HALF = S // 2
-QUANT = 256
 RUN = 4
 W_RAW_BYTES = PACK * N * 4
 
-CHUNKS = (((512, 256), (512, 192)), ((512, 320), (256, 128), (256, 128)))
+CHUNKS = (
+    ((1024, 640),),
+    ((512, 0), (512, 256)),
+    ((512, 0), (512, 0)),
+    ((512, 0), (256, 0), (256, 256)),
+)
 
 
 def round_and_interleave(nc, on_scalar, grouped, rows):
@@ -39,12 +42,16 @@ def round_and_interleave(nc, on_scalar, grouped, rows):
         nc.vector.tensor_copy(target, source)
 
 
-def quantise(nc, words, scales, grouped):
-    nc.vector.quantize_mx(out=words.bitcast(FP8X4), scales=scales, in_=grouped.rearrange("p c t -> p (c t)"))
+def quantise(nc, codes, scales, values):
+    nc.vector.quantize_mx(out=codes[:].bitcast(FP8X4), scales=scales[:], in_=values[:])
 
 
 def list_half(list_tile, h):
     return list_tile[:, h * HALF // LIST_ROWS : (h + 1) * HALF // LIST_ROWS]
+
+
+def word(picked, u):
+    return picked[:].bitcast(U32).rearrange("p (c u) -> p c u", u=2)[:, :, u]
 
 
 def tile_picked_route2_lingelu_e_kernel(tc, xT, gate, w1, offs, dst, out):
@@ -57,22 +64,24 @@ def tile_picked_route2_lingelu_e_kernel(tc, xT, gate, w1, offs, dst, out):
         offs_t = keep.tile([P, S // LIST_ROWS], U16, name="offs_t")
         dst_t = keep.tile([P, S // LIST_ROWS], U16, name="dst_t")
         placed = keep.tile([P, U], F32, name="placed", align_bytes=64)
-        all_scales = keep.tile([P, T], U8, name="all_scales", align_bytes=64)
-        all_words = [keep.tile([P, T], U32, name=f"all_words{g}", align_bytes=64) for g in range(PASSES)]
 
-        nc.vector.memset(all_scales[:].bitcast(I32), 0)
+        warm = keep.tile([P, 8], F32, name="warm")
+        warm_out = keep.tile([P, 8], F32, name="warm_out")
+        nc.vector.memset(warm[:], 0.0)
+        nc.scalar.activation(warm_out[:], warm[:], GELU)
         nc.vector.memset(placed[:], 0.0)
 
         x_raw = {}
-        for g in range(PASSES):
+        for r in range(PAIRS):
+            g, u = divmod(r, 2)
             rows = xT[g * K_PASS : (g + 1) * K_PASS, :].rearrange("(p j) t -> p j t", j=PACK)
             first = 0
-            for tokens, scalar_share in CHUNKS[g]:
-                x_raw[g, first] = keep.tile([P, PACK, tokens], F32, name=f"x_raw{g}_{first}", align_bytes=64)
-                nc.sync.dma_start(x_raw[g, first][:], rows[:, :, first : first + tokens])
-                if (g, first) == (0, 0):
-                    nc.sync.dma_start(offs_t[:], offs)
+            for tokens, vector_share in CHUNKS[r]:
+                x_raw[r, first] = keep.tile([P, 2, tokens], F32, name=f"x_raw{r}_{first}", align_bytes=64)
+                nc.sync.dma_start(x_raw[r, first][:], rows[:, 2 * u : 2 * u + 2, first : first + tokens])
                 first = first + tokens
+            if r == 0:
+                nc.sync.dma_start(offs_t[:], offs)
         w_raw = []
         for g in range(PASSES):
             w_raw.append(reused.tile([P, PACK, N], F32, name=f"w_raw{g}", align_bytes=64, offset=g * W_RAW_BYTES))
@@ -81,67 +90,82 @@ def tile_picked_route2_lingelu_e_kernel(tc, xT, gate, w1, offs, dst, out):
         nc.sync.dma_start(gate_t[:], gate)
         nc.sync.dma_start(dst_t[:], dst)
 
-        x_grouped = [keep.tile([P, T, PACK], BF16, name=f"x_grouped{g}", align_bytes=64) for g in range(PASSES)]
-        picked_words0 = keep.tile([P, S], U32, name="picked_words0", align_bytes=64)
-        for g in range(PASSES):
-            first = 0
-            for tokens, scalar_share in CHUNKS[g]:
-                grouped = x_grouped[g][:, first : first + tokens, :]
-                split = tokens - scalar_share
-                round_and_interleave(nc, True, grouped[:, split:tokens, :], x_raw[g, first][:, :, split:tokens])
-                for a in range(0, split, QUANT):
-                    b = min(a + QUANT, split)
-                    round_and_interleave(nc, False, grouped[:, a:b, :], x_raw[g, first][:, :, a:b])
-                for a in range(first, first + tokens, QUANT):
-                    cols = slice(a, a + QUANT)
-                    quantise(nc, all_words[g][:, cols], all_scales[SCALE_ROW[g] : P, cols], x_grouped[g][:, cols, :])
-                first = first + tokens
-            if g == 0:
-                nc.vector.tensor_copy(picked_words0[:], all_words[0][:].indirect(offs_t[:]))
+        pairs = [keep.tile([P, 2 * T], BF16, name=f"pairs{r}", align_bytes=64) for r in range(PAIRS)]
 
-        w_words = []
+        def round_pair(r):
+            grouped = pairs[r][:].rearrange("p (c e) -> p c e", e=2)
+            first = 0
+            for tokens, vector_share in CHUNKS[r]:
+                chunk = grouped[:, first : first + tokens, :]
+                if vector_share < tokens:
+                    round_and_interleave(
+                        nc, True, chunk[:, vector_share:tokens, :], x_raw[r, first][:, :, vector_share:tokens]
+                    )
+                if vector_share > 0:
+                    round_and_interleave(nc, False, chunk[:, 0:vector_share, :], x_raw[r, first][:, :, 0:vector_share])
+                first = first + tokens
+
+        def gather(target, r, h):
+            nc.vector.tensor_copy(target, pairs[r][:].bitcast(U32).indirect(list_half(offs_t, h)))
+
+        picked = [[None, None], [None, None]]
+        x_codes = [[None, None], [None, None]]
+        x_scales = [[None, None], [None, None]]
+        for g in range(PASSES):
+            for h in range(2):
+                if (g, h) == (1, 1):
+                    picked[g][h] = reused.tile(
+                        [P, HALF * PACK], BF16, name="picked1_1", align_bytes=64, offset=W_RAW_BYTES
+                    )
+                else:
+                    picked[g][h] = keep.tile([P, HALF * PACK], BF16, name=f"picked{g}_{h}", align_bytes=64)
+                if (g, h) == (1, 0):
+                    x_codes[g][h] = reused.tile([P, HALF], U32, name="x_codes1_0", align_bytes=64, offset=0)
+                else:
+                    x_codes[g][h] = keep.tile([P, HALF], U32, name=f"x_codes{g}_{h}", align_bytes=64)
+                x_scales[g][h] = keep.tile([P, HALF], U8, name=f"x_scales{g}_{h}", align_bytes=64)
+
+        for u in range(2):
+            round_pair(u)
+            for h in range(2):
+                gather(word(picked[0][h], u), u, h)
+        for h in range(2):
+            quantise(nc, x_codes[0][h], x_scales[0][h], picked[0][h])
+
+        parked = keep.tile([P, HALF], U32, name="parked", align_bytes=64)
+        round_pair(2)
+        gather(word(picked[1][0], 0), 2, 0)
+        gather(parked[:], 2, 1)
+
+        w_codes = []
         w_scales = []
 
         def quantise_weights(g):
-            w_grouped = keep.tile([P, N, PACK], BF16, name=f"w_grouped{g}", align_bytes=64)
-            round_and_interleave(nc, True, w_grouped[:], w_raw[g][:])
-            w_words.append(keep.tile([P, N], U32, name=f"w_words{g}", align_bytes=64))
+            w_grouped = keep.tile([P, N * PACK], BF16, name=f"w_grouped{g}", align_bytes=64)
+            round_and_interleave(nc, True, w_grouped[:].rearrange("p (m t) -> p m t", t=PACK), w_raw[g][:])
+            w_codes.append(keep.tile([P, N], U32, name=f"w_codes{g}", align_bytes=64))
             w_scales.append(keep.tile([P, N], U8, name=f"w_scales{g}", align_bytes=64))
-            quantise(nc, w_words[g][:], w_scales[g][:], w_grouped[:])
+            quantise(nc, w_codes[g], w_scales[g], w_grouped)
 
-        def gather_scales(h, tile):
-            nc.vector.tensor_copy(tile[:], all_scales[:].indirect(list_half(offs_t, h)))
-
-        def gather_words1(h, tile):
-            nc.vector.tensor_copy(tile[:], all_words[1][:].indirect(list_half(offs_t, h)))
-
-        words_bytes = HALF * 4
-        picked_scales = [
-            keep.tile([P, HALF], U8, name="picked_scales0", align_bytes=64),
-            reused.tile([P, HALF], U8, name="picked_scales1", align_bytes=64, offset=W_RAW_BYTES + words_bytes),
-        ]
-        picked_words1 = [
-            reused.tile([P, HALF], U32, name=f"picked_words1_{h}", align_bytes=64, offset=h * W_RAW_BYTES)
-            for h in range(2)
-        ]
-        gather_scales(0, picked_scales[0])
+        round_pair(3)
+        gather(word(picked[1][0], 1), 3, 0)
         quantise_weights(0)
-        gather_words1(0, picked_words1[0])
+        quantise(nc, x_codes[1][0], x_scales[1][0], picked[1][0])
         quantise_weights(1)
-        gather_scales(1, picked_scales[1])
-        gather_words1(1, picked_words1[1])
+        nc.scalar.copy(word(picked[1][1], 0), parked[:])
+        gather(word(picked[1][1], 1), 3, 1)
+        quantise(nc, x_codes[1][1], x_scales[1][1], picked[1][1])
 
         activated = []
         for h in range(2):
             acc = psum.tile([P, HALF], F32, name=f"acc{h}")
-            moving = (picked_words0[:, h * HALF : (h + 1) * HALF], picked_words1[h][:])
             for g in range(PASSES):
                 nc.tensor.matmul_mx(
                     out=acc[:],
-                    lhsT=w_words[g][:].bitcast(FP8X4),
+                    lhsT=w_codes[g][:].bitcast(FP8X4),
                     lhsT_scale=w_scales[g][:],
-                    rhs=moving[g].bitcast(FP8X4),
-                    rhs_scale=picked_scales[h][SCALE_ROW[g] : P, :],
+                    rhs=x_codes[g][h][:].bitcast(FP8X4),
+                    rhs_scale=x_scales[g][h][:],
                     start=(g == 0),
                     stop=(g == PASSES - 1),
                 )

from contextlib import ExitStack

import concourse.mybir as mybir

K, T, S, N, U = 1024, 1024, 512, 128, 1024
FLOPS = 2 * K * S * N

F32 = mybir.dt.float32
BF16 = mybir.dt.bfloat16
U32 = mybir.dt.uint32
U16 = mybir.dt.uint16
U8 = mybir.dt.uint8
FP8X4 = mybir.dt.float8_e4m3fn_x4
COPY = mybir.ActivationFunctionType.Copy
GELU = mybir.ActivationFunctionType.Gelu_apprx_tanh
MULT = mybir.AluOpType.mult

P = 128
PACK = 4
K_PASS = P * PACK
PASSES = K // K_PASS
PAIRS = 2 * PASSES
LIST_ROWS = 16
HALF = S // 2
RUN = 4
W_RAW_BYTES = PACK * N * 4

CHUNKS = (
    ((1024, 640),),
    ((512, 0), (512, 256)),
    ((512, 0), (512, 0)),
    ((512, 0), (256, 0), (256, 256)),
)


def round_and_interleave(nc, on_scalar, grouped, rows):
    target = grouped.rearrange("p (c i) t -> p c t i", i=RUN)
    source = rows.rearrange("p t (c i) -> p c t i", i=RUN)
    if on_scalar:
        nc.scalar.activation(target, source, COPY)
    else:
        nc.vector.tensor_copy(target, source)


def quantise(nc, codes, scales, values):
    nc.vector.quantize_mx(out=codes[:].bitcast(FP8X4), scales=scales[:], in_=values[:])


def list_half(list_tile, h):
    return list_tile[:, h * HALF // LIST_ROWS : (h + 1) * HALF // LIST_ROWS]


def word(picked, u):
    return picked[:].bitcast(U32).rearrange("p (c u) -> p c u", u=2)[:, :, u]


def tile_picked_route2_lingelu_e_kernel(tc, xT, gate, w1, offs, dst, out):
    nc = tc.nc
    with ExitStack() as ctx:
        keep = ctx.enter_context(tc.tile_pool(name="keep", bufs=1))
        reused = ctx.enter_context(tc.tile_pool(name="reused", bufs=1))
        psum = ctx.enter_context(tc.psum_pool(name="psum", bufs=1))

        offs_t = keep.tile([P, S // LIST_ROWS], U16, name="offs_t")
        dst_t = keep.tile([P, S // LIST_ROWS], U16, name="dst_t")
        placed = keep.tile([P, U], F32, name="placed", align_bytes=64)

        warm = keep.tile([P, 8], F32, name="warm")
        warm_out = keep.tile([P, 8], F32, name="warm_out")
        nc.vector.memset(warm[:], 0.0)
        nc.scalar.activation(warm_out[:], warm[:], GELU)
        nc.vector.memset(placed[:], 0.0)

        x_raw = {}
        for r in range(PAIRS):
            g, u = divmod(r, 2)
            rows = xT[g * K_PASS : (g + 1) * K_PASS, :].rearrange("(p j) t -> p j t", j=PACK)
            first = 0
            for tokens, vector_share in CHUNKS[r]:
                x_raw[r, first] = keep.tile([P, 2, tokens], F32, name=f"x_raw{r}_{first}", align_bytes=64)
                nc.sync.dma_start(x_raw[r, first][:], rows[:, 2 * u : 2 * u + 2, first : first + tokens])
                first = first + tokens
            if r == 0:
                nc.sync.dma_start(offs_t[:], offs)
        w_raw = []
        for g in range(PASSES):
            w_raw.append(reused.tile([P, PACK, N], F32, name=f"w_raw{g}", align_bytes=64, offset=g * W_RAW_BYTES))
            nc.sync.dma_start(w_raw[g][:], w1[g * K_PASS : (g + 1) * K_PASS, :].rearrange("(p j) m -> p j m", j=PACK))
        gate_t = keep.tile([P, S], F32, name="gate_t", align_bytes=64)
        nc.sync.dma_start(gate_t[:], gate)
        nc.sync.dma_start(dst_t[:], dst)

        pairs = [keep.tile([P, 2 * T], BF16, name=f"pairs{r}", align_bytes=64) for r in range(PAIRS)]

        def round_pair(r):
            grouped = pairs[r][:].rearrange("p (c e) -> p c e", e=2)
            first = 0
            for tokens, vector_share in CHUNKS[r]:
                chunk = grouped[:, first : first + tokens, :]
                if vector_share < tokens:
                    round_and_interleave(
                        nc, True, chunk[:, vector_share:tokens, :], x_raw[r, first][:, :, vector_share:tokens]
                    )
                if vector_share > 0:
                    round_and_interleave(nc, False, chunk[:, 0:vector_share, :], x_raw[r, first][:, :, 0:vector_share])
                first = first + tokens

        def gather(target, r, h):
            nc.vector.tensor_copy(target, pairs[r][:].bitcast(U32).indirect(list_half(offs_t, h)))

        picked = [[None, None], [None, None]]
        x_codes = [[None, None], [None, None]]
        x_scales = [[None, None], [None, None]]
        for g in range(PASSES):
            for h in range(2):
                if (g, h) == (1, 1):
                    picked[g][h] = reused.tile(
                        [P, HALF * PACK], BF16, name="picked1_1", align_bytes=64, offset=W_RAW_BYTES
                    )
                else:
                    picked[g][h] = keep.tile([P, HALF * PACK], BF16, name=f"picked{g}_{h}", align_bytes=64)
                if (g, h) == (1, 0):
                    x_codes[g][h] = reused.tile([P, HALF], U32, name="x_codes1_0", align_bytes=64, offset=0)
                else:
                    x_codes[g][h] = keep.tile([P, HALF], U32, name=f"x_codes{g}_{h}", align_bytes=64)
                x_scales[g][h] = keep.tile([P, HALF], U8, name=f"x_scales{g}_{h}", align_bytes=64)

        for u in range(2):
            round_pair(u)
            for h in range(2):
                gather(word(picked[0][h], u), u, h)
        for h in range(2):
            quantise(nc, x_codes[0][h], x_scales[0][h], picked[0][h])

        parked = keep.tile([P, HALF], U32, name="parked", align_bytes=64)
        round_pair(2)
        gather(word(picked[1][0], 0), 2, 0)
        gather(parked[:], 2, 1)

        w_codes = []
        w_scales = []

        def quantise_weights(g):
            w_grouped = keep.tile([P, N * PACK], BF16, name=f"w_grouped{g}", align_bytes=64)
            round_and_interleave(nc, True, w_grouped[:].rearrange("p (m t) -> p m t", t=PACK), w_raw[g][:])
            w_codes.append(keep.tile([P, N], U32, name=f"w_codes{g}", align_bytes=64))
            w_scales.append(keep.tile([P, N], U8, name=f"w_scales{g}", align_bytes=64))
            quantise(nc, w_codes[g], w_scales[g], w_grouped)

        round_pair(3)
        gather(word(picked[1][0], 1), 3, 0)
        quantise_weights(0)
        quantise(nc, x_codes[1][0], x_scales[1][0], picked[1][0])
        quantise_weights(1)
        nc.scalar.copy(word(picked[1][1], 0), parked[:])
        gather(word(picked[1][1], 1), 3, 1)
        quantise(nc, x_codes[1][1], x_scales[1][1], picked[1][1])

        activated = []
        for h in range(2):
            acc = psum.tile([P, HALF], F32, name=f"acc{h}")
            for g in range(PASSES):
                nc.tensor.matmul_mx(
                    out=acc[:],
                    lhsT=w_codes[g][:].bitcast(FP8X4),
                    lhsT_scale=w_scales[g][:],
                    rhs=x_codes[g][h][:].bitcast(FP8X4),
                    rhs_scale=x_scales[g][h][:],
                    start=(g == 0),
                    stop=(g == PASSES - 1),
                )
            activated.append(keep.tile([P, HALF], F32, name=f"activated{h}", align_bytes=64))
            nc.scalar.activation(activated[h][:], acc[:], GELU)

        for h in range(2):
            nc.vector.tensor_tensor(
                placed[:].indirect(list_half(dst_t, h)), activated[h][:], gate_t[:, h * HALF : (h + 1) * HALF], MULT
            )
        nc.sync.dma_start(out, placed[:])
